import numpy as np
import ml_dtypes


def mxq(x, axis, fmt="e4m3"):
    dtype, down = {"e4m3": (ml_dtypes.float8_e4m3fn, 7), "e5m2": (ml_dtypes.float8_e5m2, 14)}[fmt]
    v = np.moveaxis(np.asarray(x, np.float32).astype(ml_dtypes.bfloat16).astype(np.float64), axis, -1)
    blocks = v.reshape(v.shape[:-1] + (-1, 32))
    amax = np.abs(blocks).max(-1, keepdims=True)
    byte = np.maximum(np.where(amax > 0, np.frexp(amax)[1] - 1 + 127, 0) - down, 1)
    scale = np.exp2(byte - 127.0)
    codes = (blocks / scale).astype(np.float32).astype(dtype).astype(np.float64)
    return np.moveaxis((codes * scale).reshape(v.shape), -1, axis)


WIDE = False


def mx_kscale(k):
    if not WIDE:
        return np.ones(k)
    levels = np.array([10, -10, 5, -5, 0])
    if k % 512:
        return np.exp2(np.random.permutation(np.resize(levels, k // 32))).repeat(32)
    a = np.empty((k // 512, 16))
    for p in range(k // 512):
        a[p, :8] = np.random.permutation(np.resize(levels, 8))
        for g in range(8):
            far = levels[np.abs(levels - a[p, g]) >= 10]
            a[p, g + 8] = far[np.random.randint(len(far))]
    return np.exp2(a.ravel()).repeat(32)


def f64(x):
    return np.asarray(x).astype(np.float64)


def striped(idx):
    return np.tile(np.asarray(idx).reshape(-1, 16).T, (8, 1)).astype(np.uint16)


def unstriped(offs):
    return offs[:16].T.reshape(-1).astype(np.int64)


E2M1 = np.array([0.0, 0.5, 1.0, 1.5, 2.0, 3.0, 4.0, 6.0, -0.0, -0.5, -1.0, -1.5, -2.0, -3.0, -4.0, -6.0])


def pack_weight(w, fmt):
    k, n = w.shape
    w = f64(np.asarray(w, np.float32).astype(ml_dtypes.bfloat16)).reshape(k // 32, 32, n)
    amax = np.abs(w).max(1)
    if fmt == "e4m3":
        byte = np.frexp(amax)[1] - 1 + 127 - 7
    else:
        mant, ex = np.frexp(amax / 6.0)
        byte = np.where(mant > 0.5, ex, ex - 1) + 127
    byte = np.clip(np.where(amax > 0, byte, 1), 1, 254)
    scaled = (w * np.exp2(127.0 - byte)[:, None, :]).reshape(k, n).astype(np.float32)
    by_word = np.ascontiguousarray(scaled.reshape(k // 512, 128, 4, n).transpose(0, 1, 3, 2))
    if fmt == "e4m3":
        words = by_word.astype(ml_dtypes.float8_e4m3fn).view(np.uint8)
    else:
        c = by_word.astype(ml_dtypes.float4_e2m1fn).view(np.uint8) & 0xF
        words = (c[..., 0::2] | (c[..., 1::2] << 4)).reshape(k // 512, 128, 2 * n)
    return np.ascontiguousarray(words), np.ascontiguousarray(byte.astype(np.uint8).reshape(k // 512, 16, n))


def unpack_weight(words, scales, fmt):
    g, _, n = scales.shape
    words = np.ascontiguousarray(words).reshape(g, 128, n, -1)
    if fmt == "e4m3":
        vals = words.view(ml_dtypes.float8_e4m3fn).astype(np.float64)
    else:
        nib = np.empty((g, 128, n, 4), np.uint8)
        nib[..., 0::2] = words & 0xF
        nib[..., 1::2] = words >> 4
        vals = E2M1[nib]
    vals = vals * np.repeat(np.exp2(scales.astype(np.float64) - 127.0), 8, axis=1)[..., None]
    return vals.transpose(0, 1, 3, 2).reshape(g * 512, n)


def rot(x):
    y = x.reshape(-1, 2, x.shape[1])
    return np.stack([-y[:, 1], y[:, 0]], axis=1).reshape(x.shape)


D, T, I, Q, E, U = 512, 1024, 512, 128, 512, 512


def setup_inputs():
    n = np.random.standard_normal
    idx = np.random.permutation(T)[:I]
    idx2 = np.random.randint(0, U, I)
    fd = mx_kscale(D)
    fi = mx_kscale(I)
    keysp = pack_weight(n((D, T)) / fd[:, None], "e4m3")
    return {
        "query": (n((D, Q)) * 0.25 / np.sqrt(D) * fd[:, None]).astype(np.float32),
        "keys_words": keysp[0],
        "keys_scales": keysp[1],
        "size": (np.random.uniform(0.5, 2.0, (1, I)) * fi).astype(np.float32),
        "vals": (n((E, T))).astype(np.float32),
        "cosn": (np.repeat(np.round(np.cos(np.arange(E // 2)[:, None] * 0.11 + np.arange(U)[None] * 0.37) * 64) / 64, 2, axis=0)).astype(np.float32),
        "sinn": (np.repeat(np.round(np.sin(np.arange(E // 2)[:, None] * 0.11 + np.arange(U)[None] * 0.37) * 64) / 64, 2, axis=0)).astype(np.float32),
        "vsc": (np.random.uniform(0.5, 2.0, (I, 1)) / fi[:, None]).astype(np.float32),
        "offs": striped(idx),
        "offs2": striped(idx2),
    }


def reference(query, keys_words, keys_scales, size, vals, cosn, sinn, vsc, offs, offs2):
    idx = unstriped(offs)
    idx2 = unstriped(offs2)
    keysu = unpack_weight(keys_words, keys_scales, "e4m3")
    queryq = mxq(f64(query), 0, "e4m3")
    keysidxg = keysu[:, idx]
    a = queryq.T @ keysidxg
    p = np.exp(a - np.max(a, axis=1, keepdims=True))
    w = p * f64(size) / np.sum(p, axis=1, keepdims=True)
    wt = w.T
    vr = rot(f64(vals)[:, idx])
    v1 = f64(vals)[:, idx] * f64(cosn)[:, idx2] + vr * f64(sinn)[:, idx2]
    v2 = v1.T
    vv = v2 * f64(vsc)
    wtq = mxq(wt, 0, "e4m3")
    vvq = mxq(vv, 0, "e4m3")
    o = wtq.T @ vvq
    return o

@@ -1,0 +1,210 @@
+from contextlib import ExitStack
+
+import concourse.mybir as mybir
+from concourse.masks import make_identity
+
+D, T, I, Q, E, U = 512, 1024, 512, 128, 512, 512
+FLOPS = 2 * Q * D * I + 2 * Q * I * E
+
+F32 = mybir.dt.float32
+BF16 = mybir.dt.bfloat16
+I32 = mybir.dt.int32
+U32 = mybir.dt.uint32
+U16 = mybir.dt.uint16
+U8 = mybir.dt.uint8
+FP8X4 = mybir.dt.float8_e4m3fn_x4
+ALU = mybir.AluOpType
+ACT = mybir.ActivationFunctionType
+AX = mybir.AxisListType
+
+P = 128
+PACK = 4
+RUN = 8
+GROUPS = P // RUN
+HALVES = 2
+WINDOW = 704
+
+
+def dealt(ap):
+    return ap.rearrange("p (g t r) -> p t g r", g=GROUPS, t=PACK, r=RUN)
+
+
+def by_place(ap):
+    return ap.rearrange("p (t g r) -> p t g r", g=GROUPS, t=PACK, r=RUN)
+
+
+def tile_attend_turnedvalues_kernel(tc, query, keys_words, keys_scales, size, vals, cosn, sinn, vsc, offs, offs2, out):
+    nc = tc.nc
+    with ExitStack() as ctx:
+        sb = ctx.enter_context(tc.tile_pool(name="sb", bufs=1))
+        ps = ctx.enter_context(tc.psum_pool(name="ps", bufs=1))
+
+        def bank(n, name):
+            return ps.tile([P, 512], F32, tag="bank%d" % n, name=name)
+
+        tok_list = sb.tile([P, I // 16], U16, name="tok_list")
+        dist_list = sb.tile([P, I // 16], U16, name="dist_list")
+        cos_tab = [sb.tile([P, WINDOW], F32, name="cos_tab%d" % j) for j in range(HALVES)]
+        sin_tab = [sb.tile([P, WINDOW], F32, name="sin_tab%d" % j) for j in range(HALVES)]
+        val_tab = [[sb.tile([P, T], F32, name="val_tab%d%d" % (j, par)) for par in range(2)] for j in range(HALVES)]
+        key_words = sb.tile([P, T], U32, name="key_words")
+        key_bytes = sb.tile([P, T], U8, name="key_bytes")
+        q_raw = sb.tile([P, PACK, Q], F32, name="q_raw")
+        rows = sb.tile([P, P], F32, name="rows")
+        ident = sb.tile([P, P], F32, name="ident")
+        warm = sb.tile([P, 1], F32, name="warm")
+        warm_out = sb.tile([P, 1], F32, name="warm_out")
+
+        nc.vector.memset(rows[:], 0.0)
+        nc.vector.memset(key_bytes[:].bitcast(I32), 0)
+        for j in range(HALVES):
+            nc.vector.memset(cos_tab[j][:, U:], 0.0)
+            nc.vector.memset(sin_tab[j][:, U:], 0.0)
+        nc.gpsimd.memset(warm[:], 0.0)
+        make_identity(nc, ident[:])
+        nc.scalar.activation(warm_out[:], warm[:], ACT.Exp)
+
+        cos_rows = cosn.rearrange("(j p two) u -> j two p u", two=2, p=P)
+        sin_rows = sinn.rearrange("(j p two) u -> j two p u", two=2, p=P)
+        val_rows = vals.rearrange("(j p two) t -> j two p t", two=2, p=P)
+
+        nc.sync.dma_start(dist_list[:], offs2)
+        nc.sync.dma_start(cos_tab[0][:, :U], cos_rows[0, 0])
+        nc.sync.dma_start(sin_tab[0][:, :U], sin_rows[0, 0])
+        nc.sync.dma_start(rows[PACK : 2 * PACK, :], vsc.rearrange("(b p) o -> b (p o)", p=P))
+        nc.sync.dma_start(
+            rows[0:PACK, :].rearrange("t (g r) -> t g r", r=RUN),
+            size.rearrange("o (g t r) -> t (o g) r", t=PACK, r=RUN),
+        )
+        nc.sync.dma_start(cos_tab[1][:, :U], cos_rows[1, 0])
+        nc.sync.dma_start(sin_tab[1][:, :U], sin_rows[1, 0])
+        nc.sync.dma_start(tok_list[:], offs)
+        nc.sync.dma_start(key_words[:].bitcast(I32), keys_words[0].rearrange("p n t -> p (n t)").bitcast(I32))
+        for quad in range(4):
+            nc.sync.dma_start(
+                key_bytes[32 * quad : 32 * quad + 4, :].bitcast(I32),
+                keys_scales[0, 4 * quad : 4 * quad + 4, :].bitcast(I32),
+            )
+        nc.sync.dma_start(q_raw[:], query.rearrange("(p t) q -> p t q", t=PACK))
+        for j in range(HALVES):
+            for par in (1, 0):
+                nc.sync.dma_start(val_tab[j][par][:], val_rows[j, par])
+
+        cols_ps = bank(6, "cols_ps")
+        nc.tensor.transpose(cols_ps[:, :P], rows[:], ident[:])
+        cols = sb.tile([P, 2 * PACK], F32, name="cols")
+        nc.scalar.copy(cols[:], cols_ps[:, : 2 * PACK])
+
+        def scaled_turn(j):
+            cos_g = sb.tile([P, I], F32, name="cos_g%d" % j)
+            sin_g = sb.tile([P, I], F32, name="sin_g%d" % j)
+            nc.vector.tensor_copy(cos_g[:], cos_tab[j][:].indirect(dist_list[:]))
+            nc.vector.tensor_copy(sin_g[:], sin_tab[j][:].indirect(dist_list[:]))
+            there = [bank(h, "there%d%d" % (j, h)) for h in range(2)]
+            for k, g in enumerate((cos_g, sin_g)):
+                for b in range(PACK):
+                    at = (2 * (b % 2) + k) * P
+                    nc.tensor.transpose(there[b // 2][:, at : at + P], g[:, b * P : (b + 1) * P], ident[:])
+            back = [bank(2 + 2 * j + k, "back%d%d" % (j, k)) for k in range(2)]
+            for b in range(PACK):
+                scaled = sb.tile([P, 2 * P], F32, name="scaled%d%d" % (j, b))
+                at = 2 * (b % 2) * P
+                nc.scalar.activation(scaled[:], there[b // 2][:, at : at + 2 * P], ACT.Copy, scale=cols[:, PACK + b : PACK + b + 1])
+                for k in range(2):
+                    nc.tensor.transpose(back[k][:, b * P : (b + 1) * P], scaled[:, k * P : (k + 1) * P], ident[:])
+            return back
+
+        turn = [scaled_turn(j) for j in range(HALVES)]
+
+        q_bf = sb.tile([P, Q, PACK], BF16, name="q_bf", align_bytes=64)
+        nc.scalar.copy(q_bf[:], q_raw[:].rearrange("p t q -> p q t"))
+        k_words = sb.tile([P, I], U32, name="k_words", align_bytes=64)
+        k_bytes = sb.tile([P, I], U8, name="k_bytes", align_bytes=64)
+        nc.vector.tensor_copy(k_words[:], key_words[:].indirect(tok_list[:]))
+        nc.vector.tensor_copy(k_bytes[:], key_bytes[:].indirect(tok_list[:]))
+        q_words = sb.tile([P, Q], U32, name="q_words", align_bytes=64)
+        q_bytes = sb.tile([P, Q], U8, name="q_bytes", align_bytes=64)
+        nc.vector.quantize_mx(out=q_words[:].bitcast(FP8X4), scales=q_bytes[:], in_=q_bf[:].rearrange("p q t -> p (q t)"))
+        scores = bank(6, "scores")
+        nc.tensor.matmul_mx(
+            out=scores[:], lhsT=q_words[:].bitcast(FP8X4), lhsT_scale=q_bytes[:],
+            rhs=k_words[:].bitcast(FP8X4), rhs_scale=k_bytes[:], start=True, stop=True,
+        )
+
+        def gather_values(j):
+            odd = sb.tile([P, I], F32, name="odd%d" % j)
+            even = sb.tile([P, I], F32, name="even%d" % j)
+            neg_odd = sb.tile([P, I], F32, name="neg_odd%d" % j)
+            nc.vector.tensor_copy(odd[:], val_tab[j][1][:].indirect(tok_list[:]))
+            nc.scalar.activation(neg_odd[:], odd[:], ACT.Copy, scale=-1.0)
+            return odd, even, neg_odd
+
+        def gather_even(j, even):
+            nc.vector.tensor_copy(even[:], val_tab[j][0][:].indirect(tok_list[:]))
+
+        def rotate(j, par, first, second):
+            cos_b, sin_b = turn[j]
+            acc = bank(par, "acc%d%d" % (j, par))
+            for k, (v, f) in enumerate(((first, cos_b), (second, sin_b))):
+                prod = sb.tile([P, I], F32, name="prod%d%d%d" % (j, par, k))
+                nc.vector.tensor_tensor(by_place(prod[:]), dealt(v[:]), dealt(f[:]), ALU.mult)
+                for t in range(PACK):
+                    nc.tensor.matmul(
+                        acc[:, t * P : (t + 1) * P], prod[:, t * P : (t + 1) * P], ident[:],
+                        start=(k == 0 and t == 0), stop=(k == 1 and t == PACK - 1), is_transpose=True,
+                    )
+            v_bf = sb.tile([P, P, PACK], BF16, name="v_bf%d%d" % (j, par), align_bytes=64)
+            nc.scalar.copy(v_bf[:], acc[:].rearrange("p (t m) -> p m t", t=PACK))
+            return v_bf
+
+        def weigh(j, par, v_bf, sums):
+            v_words = sb.tile([P, P], U32, name="v_words%d%d" % (j, par), align_bytes=64)
+            v_bytes = sb.tile([P, P], U8, name="v_bytes%d%d" % (j, par), align_bytes=64)
+            nc.vector.quantize_mx(out=v_words[:].bitcast(FP8X4), scales=v_bytes[:], in_=v_bf[:].rearrange("p m t -> p (m t)"))
+            nc.tensor.matmul_mx(
+                out=sums[:, par * P : (par + 1) * P], lhsT=w_words[:].bitcast(FP8X4), lhsT_scale=w_bytes[:],
+                rhs=v_words[:].bitcast(FP8X4), rhs_scale=v_bytes[:], start=True, stop=True,
+            )
+
+        def store(j, sums):
+            res = sb.tile([P, P, 2], F32, name="res%d" % j)
+            nc.scalar.copy(res[:], sums[:, : 2 * P].rearrange("p (two m) -> p m two", two=2))
+            nc.sync.dma_start(out[:, j * 2 * P : (j + 1) * 2 * P], res[:].rearrange("p m two -> p (m two)"))
+
+        odd0, even0, neg0 = gather_values(0)
+        neg_max = sb.tile([P, 1], F32, name="neg_max")
+        nc.vector.tensor_reduce(neg_max[:], scores[:], AX.X, ALU.max, negate=True)
+        gather_even(0, even0)
+        prob = sb.tile([P, I], F32, name="prob")
+        total = sb.tile([P, 1], F32, name="total")
+        nc.scalar.activation(by_place(prob[:]), dealt(scores[:]), ACT.Exp, bias=neg_max[:], scale=1.0, accum_out=total[:])
+        inv = sb.tile([P, 1], F32, name="inv")
+        nc.vector.reciprocal(inv[:], total[:])
+        normed = sb.tile([P, I], F32, name="normed")
+        nc.scalar.activation(normed[:], prob[:], ACT.Copy, scale=inv[:])
+        w_ps = bank(7, "w_ps")
+        for t in range(PACK):
+            nc.tensor.transpose(w_ps[:, t * P : (t + 1) * P], normed[:, t * P : (t + 1) * P], ident[:])
+        w_bf = sb.tile([P, Q, PACK], BF16, name="w_bf", align_bytes=64)
+        for t in range(PACK):
+            nc.scalar.activation(w_bf[:, :, t], w_ps[:, t * P : (t + 1) * P], ACT.Copy, scale=cols[:, t : t + 1])
+
+        v01 = rotate(0, 1, odd0, even0)
+        v00 = rotate(0, 0, even0, neg0)
+
+        odd1, even1, neg1 = gather_values(1)
+        w_words = sb.tile([P, Q], U32, name="w_words", align_bytes=64)
+        w_bytes = sb.tile([P, Q], U8, name="w_bytes", align_bytes=64)
+        nc.vector.quantize_mx(out=w_words[:].bitcast(FP8X4), scales=w_bytes[:], in_=w_bf[:].rearrange("p q t -> p (q t)"))
+        gather_even(1, even1)
+        sums0 = bank(6, "sums0")
+        weigh(0, 1, v01, sums0)
+        weigh(0, 0, v00, sums0)
+        store(0, sums0)
+
+        v11 = rotate(1, 1, odd1, even1)
+        v10 = rotate(1, 0, even1, neg1)
+        sums1 = bank(7, "sums1")
+        weigh(1, 1, v11, sums1)
+        weigh(1, 0, v10, sums1)
+        store(1, sums1)

@@ -23,6 +23,7 @@ RUN = 8
 GROUPS = P // RUN
 HALVES = 2
 WINDOW = 704
+EVEN, ODD = 0, 1
 
 
 def dealt(ap):
@@ -69,37 +70,49 @@ def tile_attend_turnedvalues_kernel(tc, query, keys_words, keys_scales, size, va
         val_rows = vals.rearrange("(j p two) t -> j two p t", two=2, p=P)
 
         nc.sync.dma_start(dist_list[:], offs2)
-        nc.sync.dma_start(cos_tab[0][:, :U], cos_rows[0, 0])
-        nc.sync.dma_start(sin_tab[0][:, :U], sin_rows[0, 0])
+        nc.sync.dma_start(cos_tab[0][:, :U], cos_rows[0, EVEN])
+        nc.sync.dma_start(sin_tab[0][:, :U], sin_rows[0, EVEN])
         nc.sync.dma_start(rows[PACK : 2 * PACK, :], vsc.rearrange("(b p) o -> b (p o)", p=P))
         nc.sync.dma_start(
             rows[0:PACK, :].rearrange("t (g r) -> t g r", r=RUN),
             size.rearrange("o (g t r) -> t (o g) r", t=PACK, r=RUN),
         )
-        nc.sync.dma_start(cos_tab[1][:, :U], cos_rows[1, 0])
-        nc.sync.dma_start(sin_tab[1][:, :U], sin_rows[1, 0])
+        nc.sync.dma_start(q_raw[:], query.rearrange("(p t) q -> p t q", t=PACK))
         nc.sync.dma_start(tok_list[:], offs)
+        nc.sync.dma_start(val_tab[0][ODD][:], val_rows[0, ODD])
+        nc.sync.dma_start(cos_tab[1][:, :U], cos_rows[1, EVEN])
+        nc.sync.dma_start(sin_tab[1][:, :U], sin_rows[1, EVEN])
         nc.sync.dma_start(key_words[:].bitcast(I32), keys_words[0].rearrange("p n t -> p (n t)").bitcast(I32))
         for quad in range(4):
             nc.sync.dma_start(
                 key_bytes[32 * quad : 32 * quad + 4, :].bitcast(I32),
                 keys_scales[0, 4 * quad : 4 * quad + 4, :].bitcast(I32),
             )
-        nc.sync.dma_start(q_raw[:], query.rearrange("(p t) q -> p t q", t=PACK))
+        nc.sync.dma_start(val_tab[1][ODD][:], val_rows[1, ODD])
         for j in range(HALVES):
-            for par in (1, 0):
-                nc.sync.dma_start(val_tab[j][par][:], val_rows[j, par])
+            nc.sync.dma_start(val_tab[j][EVEN][:], val_rows[j, EVEN])
 
         cols_ps = bank(6, "cols_ps")
         nc.tensor.transpose(cols_ps[:, :P], rows[:], ident[:])
         cols = sb.tile([P, 2 * PACK], F32, name="cols")
         nc.scalar.copy(cols[:], cols_ps[:, : 2 * PACK])
+        size_ps = bank(7, "size_ps")
+        for t in range(PACK):
+            nc.tensor.transpose(size_ps[:, t * P : (t + 1) * P], cols[:, t : t + 1].to_broadcast([P, P]), ident[:])
+        size_all = sb.tile([P, I], F32, name="size_all")
+        nc.scalar.copy(size_all[:], size_ps[:])
+
+        q_bf = sb.tile([P, Q, PACK], BF16, name="q_bf", align_bytes=64)
+        nc.scalar.copy(q_bf[:], q_raw[:].rearrange("p t q -> p q t"))
+
+        def gather(name, table, offsets, dtype=F32):
+            picked = sb.tile([P, I], dtype, name=name, align_bytes=64)
+            nc.vector.tensor_copy(picked[:], table[:].indirect(offsets[:]))
+            return picked
 
         def scaled_turn(j):
-            cos_g = sb.tile([P, I], F32, name="cos_g%d" % j)
-            sin_g = sb.tile([P, I], F32, name="sin_g%d" % j)
-            nc.vector.tensor_copy(cos_g[:], cos_tab[j][:].indirect(dist_list[:]))
-            nc.vector.tensor_copy(sin_g[:], sin_tab[j][:].indirect(dist_list[:]))
+            cos_g = gather("cos_g%d" % j, cos_tab[j], dist_list)
+            sin_g = gather("sin_g%d" % j, sin_tab[j], dist_list)
             there = [bank(h, "there%d%d" % (j, h)) for h in range(2)]
             for k, g in enumerate((cos_g, sin_g)):
                 for b in range(PACK):
@@ -114,56 +127,50 @@ def tile_attend_turnedvalues_kernel(tc, query, keys_words, keys_scales, size, va
                     nc.tensor.transpose(back[k][:, b * P : (b + 1) * P], scaled[:, k * P : (k + 1) * P], ident[:])
             return back
 
-        turn = [scaled_turn(j) for j in range(HALVES)]
+        def deal(name, src, factor):
+            dst = sb.tile([P, I], F32, name=name)
+            nc.scalar.activation(by_place(dst[:]), dealt(src[:]), ACT.Copy, scale=factor)
+            return dst
 
-        q_bf = sb.tile([P, Q, PACK], BF16, name="q_bf", align_bytes=64)
-        nc.scalar.copy(q_bf[:], q_raw[:].rearrange("p t q -> p q t"))
-        k_words = sb.tile([P, I], U32, name="k_words", align_bytes=64)
-        k_bytes = sb.tile([P, I], U8, name="k_bytes", align_bytes=64)
-        nc.vector.tensor_copy(k_words[:], key_words[:].indirect(tok_list[:]))
-        nc.vector.tensor_copy(k_bytes[:], key_bytes[:].indirect(tok_list[:]))
-        q_words = sb.tile([P, Q], U32, name="q_words", align_bytes=64)
-        q_bytes = sb.tile([P, Q], U8, name="q_bytes", align_bytes=64)
-        nc.vector.quantize_mx(out=q_words[:].bitcast(FP8X4), scales=q_bytes[:], in_=q_bf[:].rearrange("p q t -> p (q t)"))
-        scores = bank(6, "scores")
-        nc.tensor.matmul_mx(
-            out=scores[:], lhsT=q_words[:].bitcast(FP8X4), lhsT_scale=q_bytes[:],
-            rhs=k_words[:].bitcast(FP8X4), rhs_scale=k_bytes[:], start=True, stop=True,
-        )
+        def odd_products(j, neg_odd, neg_cos, sin_d):
+            to_even = sb.tile([P, I], F32, name="odd_sin%d" % j)
+            to_odd = sb.tile([P, I], F32, name="odd_cos%d" % j)
+            nc.gpsimd.tensor_tensor(to_odd[:], neg_odd[:], neg_cos[:], ALU.mult)
+            nc.gpsimd.tensor_tensor(to_even[:], neg_odd[:], sin_d[:], ALU.mult)
+            return to_even, to_odd
 
-        def gather_values(j):
-            odd = sb.tile([P, I], F32, name="odd%d" % j)
-            even = sb.tile([P, I], F32, name="even%d" % j)
-            neg_odd = sb.tile([P, I], F32, name="neg_odd%d" % j)
-            nc.vector.tensor_copy(odd[:], val_tab[j][1][:].indirect(tok_list[:]))
-            nc.scalar.activation(neg_odd[:], odd[:], ACT.Copy, scale=-1.0)
-            return odd, even, neg_odd
+        def add_turned(acc, prod, places, first):
+            for t in places:
+                nc.tensor.matmul(
+                    acc[:, t * P : (t + 1) * P], prod[:, t * P : (t + 1) * P], ident[:],
+                    start=(first and t == 0), stop=(not first and t == PACK - 1), is_transpose=True,
+                )
 
-        def gather_even(j, even):
-            nc.vector.tensor_copy(even[:], val_tab[j][0][:].indirect(tok_list[:]))
-
-        def rotate(j, par, first, second):
-            cos_b, sin_b = turn[j]
-            acc = bank(par, "acc%d%d" % (j, par))
-            for k, (v, f) in enumerate(((first, cos_b), (second, sin_b))):
-                prod = sb.tile([P, I], F32, name="prod%d%d%d" % (j, par, k))
-                nc.vector.tensor_tensor(by_place(prod[:]), dealt(v[:]), dealt(f[:]), ALU.mult)
-                for t in range(PACK):
-                    nc.tensor.matmul(
-                        acc[:, t * P : (t + 1) * P], prod[:, t * P : (t + 1) * P], ident[:],
-                        start=(k == 0 and t == 0), stop=(k == 1 and t == PACK - 1), is_transpose=True,
-                    )
+        def rotate(j, par, n, odd_term, even_vals, factor, cuts):
+            acc = bank(n, "acc%d%d" % (j, par))
+            add_turned(acc, odd_term, range(PACK), True)
+            step = PACK // cuts
+            for t0 in range(0, PACK, step):
+                prod = sb.tile([P, I], F32, name="prod%d%d%d" % (j, par, t0))
+                nc.vector.tensor_tensor(
+                    by_place(prod[:])[:, t0 : t0 + step], dealt(even_vals[:])[:, t0 : t0 + step],
+                    dealt(factor[:])[:, t0 : t0 + step], ALU.mult,
+                )
+                add_turned(acc, prod, range(t0, t0 + step), False)
             v_bf = sb.tile([P, P, PACK], BF16, name="v_bf%d%d" % (j, par), align_bytes=64)
             nc.scalar.copy(v_bf[:], acc[:].rearrange("p (t m) -> p m t", t=PACK))
             return v_bf
 
-        def weigh(j, par, v_bf, sums):
-            v_words = sb.tile([P, P], U32, name="v_words%d%d" % (j, par), align_bytes=64)
-            v_bytes = sb.tile([P, P], U8, name="v_bytes%d%d" % (j, par), align_bytes=64)
-            nc.vector.quantize_mx(out=v_words[:].bitcast(FP8X4), scales=v_bytes[:], in_=v_bf[:].rearrange("p m t -> p (m t)"))
+        def quantise(name, src):
+            words = sb.tile([P, P], U32, name=name + "_words", align_bytes=64)
+            scales = sb.tile([P, P], U8, name=name + "_bytes", align_bytes=64)
+            nc.vector.quantize_mx(out=words[:].bitcast(FP8X4), scales=scales[:], in_=src[:].rearrange("p c t -> p (c t)"))
+            return words, scales
+
+        def product(dst, lhs, rhs):
             nc.tensor.matmul_mx(
-                out=sums[:, par * P : (par + 1) * P], lhsT=w_words[:].bitcast(FP8X4), lhsT_scale=w_bytes[:],
-                rhs=v_words[:].bitcast(FP8X4), rhs_scale=v_bytes[:], start=True, stop=True,
+                out=dst, lhsT=lhs[0][:].bitcast(FP8X4), lhsT_scale=lhs[1][:],
+                rhs=rhs[0][:].bitcast(FP8X4), rhs_scale=rhs[1][:], start=True, stop=True,
             )
 
         def store(j, sums):
@@ -171,40 +178,54 @@ def tile_attend_turnedvalues_kernel(tc, query, keys_words, keys_scales, size, va
             nc.scalar.copy(res[:], sums[:, : 2 * P].rearrange("p (two m) -> p m two", two=2))
             nc.sync.dma_start(out[:, j * 2 * P : (j + 1) * 2 * P], res[:].rearrange("p m two -> p (m two)"))
 
-        odd0, even0, neg0 = gather_values(0)
+        cos0, sin0 = scaled_turn(0)
+        odd0 = gather("odd0", val_tab[0][ODD], tok_list)
+        q_mx = quantise("q", q_bf)
+        neg_odd0 = deal("neg_odd0", odd0, -1.0)
+        terms0 = odd_products(0, neg_odd0, deal("neg_cos0", cos0, -1.0), deal("sin_d0", sin0, 1.0))
+
+        cos1, sin1 = scaled_turn(1)
+        neg_cos1 = deal("neg_cos1", cos1, -1.0)
+        sin_d1 = deal("sin_d1", sin1, 1.0)
+
+        k_mx = (gather("k_words", key_words, tok_list, U32), gather("k_bytes", key_bytes, tok_list, U8))
+        scores = bank(6, "scores")
+        product(scores[:], q_mx, k_mx)
+
+        odd1 = gather("odd1", val_tab[1][ODD], tok_list)
+        neg_odd1 = deal("neg_odd1", odd1, -1.0)
         neg_max = sb.tile([P, 1], F32, name="neg_max")
         nc.vector.tensor_reduce(neg_max[:], scores[:], AX.X, ALU.max, negate=True)
-        gather_even(0, even0)
+        even0 = gather("even0", val_tab[0][EVEN], tok_list)
         prob = sb.tile([P, I], F32, name="prob")
         total = sb.tile([P, 1], F32, name="total")
         nc.scalar.activation(by_place(prob[:]), dealt(scores[:]), ACT.Exp, bias=neg_max[:], scale=1.0, accum_out=total[:])
+        sized = sb.tile([P, I], F32, name="sized")
+        nc.gpsimd.tensor_tensor(sized[:], prob[:], size_all[:], ALU.mult)
+        terms1 = odd_products(1, neg_odd1, neg_cos1, sin_d1)
         inv = sb.tile([P, 1], F32, name="inv")
         nc.vector.reciprocal(inv[:], total[:])
         normed = sb.tile([P, I], F32, name="normed")
-        nc.scalar.activation(normed[:], prob[:], ACT.Copy, scale=inv[:])
+        nc.scalar.activation(normed[:], sized[:], ACT.Copy, scale=inv[:])
         w_ps = bank(7, "w_ps")
         for t in range(PACK):
             nc.tensor.transpose(w_ps[:, t * P : (t + 1) * P], normed[:, t * P : (t + 1) * P], ident[:])
         w_bf = sb.tile([P, Q, PACK], BF16, name="w_bf", align_bytes=64)
-        for t in range(PACK):
-            nc.scalar.activation(w_bf[:, :, t], w_ps[:, t * P : (t + 1) * P], ACT.Copy, scale=cols[:, t : t + 1])
+        nc.scalar.copy(w_bf[:], w_ps[:].rearrange("p (t q) -> p q t", t=PACK))
 
-        v01 = rotate(0, 1, odd0, even0)
-        v00 = rotate(0, 0, even0, neg0)
+        v01 = rotate(0, ODD, 0, terms0[ODD], even0, sin0, 1)
+        v00 = rotate(0, EVEN, 1, terms0[EVEN], even0, cos0, 1)
 
-        odd1, even1, neg1 = gather_values(1)
-        w_words = sb.tile([P, Q], U32, name="w_words", align_bytes=64)
-        w_bytes = sb.tile([P, Q], U8, name="w_bytes", align_bytes=64)
-        nc.vector.quantize_mx(out=w_words[:].bitcast(FP8X4), scales=w_bytes[:], in_=w_bf[:].rearrange("p q t -> p (q t)"))
-        gather_even(1, even1)
+        even1 = gather("even1", val_tab[1][EVEN], tok_list)
+        v11 = rotate(1, ODD, 3, terms1[ODD], even1, sin1, 1)
+        v10 = rotate(1, EVEN, 2, terms1[EVEN], even1, cos1, 2)
+
+        w_mx = quantise("w", w_bf)
         sums0 = bank(6, "sums0")
-        weigh(0, 1, v01, sums0)
-        weigh(0, 0, v00, sums0)
-        store(0, sums0)
-
-        v11 = rotate(1, 1, odd1, even1)
-        v10 = rotate(1, 0, even1, neg1)
+        product(sums0[:, ODD * P : (ODD + 1) * P], w_mx, quantise("v01", v01))
+        product(sums0[:, EVEN * P : (EVEN + 1) * P], w_mx, quantise("v00", v00))
         sums1 = bank(7, "sums1")
-        weigh(1, 1, v11, sums1)
-        weigh(1, 0, v10, sums1)
+        product(sums1[:, ODD * P : (ODD + 1) * P], w_mx, quantise("v11", v11))
+        store(0, sums0)
+        product(sums1[:, EVEN * P : (EVEN + 1) * P], w_mx, quantise("v10", v10))
         store(1, sums1)

@@ -43,12 +43,16 @@ def tile_attend_turnedvalues_kernel(tc, query, keys_words, keys_scales, size, va
         def bank(n, name):
             return ps.tile([P, 512], F32, tag="bank%d" % n, name=name)
 
+        def two_banks(name):
+            both = ps.tile([P, 2, 512], F32, tag="bank0", name=name)
+            return [both[:, 0, :], both[:, 1, :]]
+
         tok_list = sb.tile([P, I // 16], U16, name="tok_list")
         dist_list = sb.tile([P, I // 16], U16, name="dist_list")
-        cos_tab = [sb.tile([P, WINDOW], F32, name="cos_tab%d" % j) for j in range(HALVES)]
-        sin_tab = [sb.tile([P, WINDOW], F32, name="sin_tab%d" % j) for j in range(HALVES)]
-        val_tab = [[sb.tile([P, T], F32, name="val_tab%d%d" % (j, par)) for par in range(2)] for j in range(HALVES)]
-        key_words = sb.tile([P, T], U32, name="key_words")
+        cos_tab = [sb.tile([P, WINDOW], F32, name="cos_tab%d" % j, align_bytes=64) for j in range(HALVES)]
+        sin_tab = [sb.tile([P, WINDOW], F32, name="sin_tab%d" % j, align_bytes=64) for j in range(HALVES)]
+        val_tab = [[sb.tile([P, T], F32, name="val_tab%d%d" % (j, par), align_bytes=64) for par in range(2)] for j in range(HALVES)]
+        key_words = sb.tile([P, T], U32, name="key_words", align_bytes=64)
         key_bytes = sb.tile([P, T], U8, name="key_bytes")
         q_raw = sb.tile([P, PACK, Q], F32, name="q_raw")
         rows = sb.tile([P, P], F32, name="rows")
@@ -56,7 +60,7 @@ def tile_attend_turnedvalues_kernel(tc, query, keys_words, keys_scales, size, va
         warm = sb.tile([P, 1], F32, name="warm")
         warm_out = sb.tile([P, 1], F32, name="warm_out")
 
-        nc.vector.memset(rows[:], 0.0)
+        nc.gpsimd.memset(rows[:], 0.0)
         nc.vector.memset(key_bytes[:].bitcast(I32), 0)
         for j in range(HALVES):
             nc.vector.memset(cos_tab[j][:, U:], 0.0)
@@ -71,17 +75,18 @@ def tile_attend_turnedvalues_kernel(tc, query, keys_words, keys_scales, size, va
 
         nc.sync.dma_start(dist_list[:], offs2)
         nc.sync.dma_start(cos_tab[0][:, :U], cos_rows[0, EVEN])
-        nc.sync.dma_start(sin_tab[0][:, :U], sin_rows[0, EVEN])
-        nc.sync.dma_start(rows[PACK : 2 * PACK, :], vsc.rearrange("(b p) o -> b (p o)", p=P))
+        nc.sync.dma_start(rows[0:PACK, :], vsc.rearrange("(b p) o -> b (p o)", p=P))
         nc.sync.dma_start(
-            rows[0:PACK, :].rearrange("t (g r) -> t g r", r=RUN),
+            rows[PACK : 2 * PACK, :].rearrange("t (g r) -> t g r", r=RUN),
             size.rearrange("o (g t r) -> t (o g) r", t=PACK, r=RUN),
         )
+        nc.sync.dma_start(sin_tab[0][:, :U], sin_rows[0, EVEN])
         nc.sync.dma_start(q_raw[:], query.rearrange("(p t) q -> p t q", t=PACK))
         nc.sync.dma_start(tok_list[:], offs)
         nc.sync.dma_start(val_tab[0][ODD][:], val_rows[0, ODD])
         nc.sync.dma_start(cos_tab[1][:, :U], cos_rows[1, EVEN])
         nc.sync.dma_start(sin_tab[1][:, :U], sin_rows[1, EVEN])
+        nc.sync.dma_start(val_tab[0][EVEN][:], val_rows[0, EVEN])
         nc.sync.dma_start(key_words[:].bitcast(I32), keys_words[0].rearrange("p n t -> p (n t)").bitcast(I32))
         for quad in range(4):
             nc.sync.dma_start(
@@ -89,40 +94,38 @@ def tile_attend_turnedvalues_kernel(tc, query, keys_words, keys_scales, size, va
                 keys_scales[0, 4 * quad : 4 * quad + 4, :].bitcast(I32),
             )
         nc.sync.dma_start(val_tab[1][ODD][:], val_rows[1, ODD])
-        for j in range(HALVES):
-            nc.sync.dma_start(val_tab[j][EVEN][:], val_rows[j, EVEN])
+        nc.sync.dma_start(val_tab[1][EVEN][:], val_rows[1, EVEN])
 
-        cols_ps = bank(6, "cols_ps")
+        cols_ps = bank(0, "cols_ps")
         nc.tensor.transpose(cols_ps[:, :P], rows[:], ident[:])
         cols = sb.tile([P, 2 * PACK], F32, name="cols")
         nc.scalar.copy(cols[:], cols_ps[:, : 2 * PACK])
-        size_ps = bank(7, "size_ps")
-        for t in range(PACK):
-            nc.tensor.transpose(size_ps[:, t * P : (t + 1) * P], cols[:, t : t + 1].to_broadcast([P, P]), ident[:])
-        size_all = sb.tile([P, I], F32, name="size_all")
-        nc.scalar.copy(size_all[:], size_ps[:])
 
-        q_bf = sb.tile([P, Q, PACK], BF16, name="q_bf", align_bytes=64)
-        nc.scalar.copy(q_bf[:], q_raw[:].rearrange("p t q -> p q t"))
-
-        def gather(name, table, offsets, dtype=F32):
-            picked = sb.tile([P, I], dtype, name=name, align_bytes=64)
+        def gather(name, table, offsets, dtype=F32, tag=None):
+            picked = sb.tile([P, I], dtype, name=name, tag=tag or name, align_bytes=64)
             nc.vector.tensor_copy(picked[:], table[:].indirect(offsets[:]))
             return picked
 
-        def scaled_turn(j):
-            cos_g = gather("cos_g%d" % j, cos_tab[j], dist_list)
-            sin_g = gather("sin_g%d" % j, sin_tab[j], dist_list)
-            there = [bank(h, "there%d%d" % (j, h)) for h in range(2)]
-            for k, g in enumerate((cos_g, sin_g)):
+        def gather_dealt(name, table, tag=None):
+            picked = sb.tile([P, I], F32, name=name, tag=tag or name, align_bytes=64)
+            nc.vector.tensor_copy(
+                picked[:].bitcast(U32).rearrange("p (t g r) -> p g t r", g=GROUPS, t=PACK, r=RUN),
+                table[:].bitcast(U32).indirect(tok_list[:]),
+            )
+            return picked
+
+        def scaled_factors(j):
+            picked = [gather("cos%d" % j, cos_tab[j], dist_list), gather("sin%d" % j, sin_tab[j], dist_list)]
+            there = two_banks("there%d" % j)
+            for k in range(2):
                 for b in range(PACK):
                     at = (2 * (b % 2) + k) * P
-                    nc.tensor.transpose(there[b // 2][:, at : at + P], g[:, b * P : (b + 1) * P], ident[:])
+                    nc.tensor.transpose(there[b // 2][:, at : at + P], picked[k][:, b * P : (b + 1) * P], ident[:])
             back = [bank(2 + 2 * j + k, "back%d%d" % (j, k)) for k in range(2)]
             for b in range(PACK):
                 scaled = sb.tile([P, 2 * P], F32, name="scaled%d%d" % (j, b))
                 at = 2 * (b % 2) * P
-                nc.scalar.activation(scaled[:], there[b // 2][:, at : at + 2 * P], ACT.Copy, scale=cols[:, PACK + b : PACK + b + 1])
+                nc.scalar.activation(scaled[:], there[b // 2][:, at : at + 2 * P], ACT.Copy, scale=cols[:, b : b + 1])
                 for k in range(2):
                     nc.tensor.transpose(back[k][:, b * P : (b + 1) * P], scaled[:, k * P : (k + 1) * P], ident[:])
             return back
@@ -132,12 +135,10 @@ def tile_attend_turnedvalues_kernel(tc, query, keys_words, keys_scales, size, va
             nc.scalar.activation(by_place(dst[:]), dealt(src[:]), ACT.Copy, scale=factor)
             return dst
 
-        def odd_products(j, neg_odd, neg_cos, sin_d):
-            to_even = sb.tile([P, I], F32, name="odd_sin%d" % j)
-            to_odd = sb.tile([P, I], F32, name="odd_cos%d" % j)
-            nc.gpsimd.tensor_tensor(to_odd[:], neg_odd[:], neg_cos[:], ALU.mult)
-            nc.gpsimd.tensor_tensor(to_even[:], neg_odd[:], sin_d[:], ALU.mult)
-            return to_even, to_odd
+        def pool_product(name, a, b):
+            prod = sb.tile([P, I], F32, name=name)
+            nc.gpsimd.tensor_tensor(prod[:], a[:], b[:], ALU.mult)
+            return prod
 
         def add_turned(acc, prod, places, first):
             for t in places:
@@ -146,86 +147,117 @@ def tile_attend_turnedvalues_kernel(tc, query, keys_words, keys_scales, size, va
                     start=(first and t == 0), stop=(not first and t == PACK - 1), is_transpose=True,
                 )
 
-        def rotate(j, par, n, odd_term, even_vals, factor, cuts):
-            acc = bank(n, "acc%d%d" % (j, par))
-            add_turned(acc, odd_term, range(PACK), True)
+        def vector_term(name, acc, values, factor, cuts, first, tags):
             step = PACK // cuts
             for t0 in range(0, PACK, step):
-                prod = sb.tile([P, I], F32, name="prod%d%d%d" % (j, par, t0))
+                prod = sb.tile([P, I], F32, name="%s_%d" % (name, t0), tag=tags[t0 // step], align_bytes=64)
                 nc.vector.tensor_tensor(
-                    by_place(prod[:])[:, t0 : t0 + step], dealt(even_vals[:])[:, t0 : t0 + step],
+                    by_place(prod[:])[:, t0 : t0 + step], dealt(values[:])[:, t0 : t0 + step],
                     dealt(factor[:])[:, t0 : t0 + step], ALU.mult,
                 )
-                add_turned(acc, prod, range(t0, t0 + step), False)
-            v_bf = sb.tile([P, P, PACK], BF16, name="v_bf%d%d" % (j, par), align_bytes=64)
-            nc.scalar.copy(v_bf[:], acc[:].rearrange("p (t m) -> p m t", t=PACK))
-            return v_bf
+                add_turned(acc, prod, range(t0, t0 + step), first)
 
-        def quantise(name, src):
-            words = sb.tile([P, P], U32, name=name + "_words", align_bytes=64)
-            scales = sb.tile([P, P], U8, name=name + "_bytes", align_bytes=64)
-            nc.vector.quantize_mx(out=words[:].bitcast(FP8X4), scales=scales[:], in_=src[:].rearrange("p c t -> p (c t)"))
-            return words, scales
+        def quantise(words, scales, src):
+            nc.vector.quantize_mx(out=words.bitcast(FP8X4), scales=scales, in_=src.rearrange("p c t -> p (c t)"))
 
-        def product(dst, lhs, rhs):
+        def product(dst, lhs, rhs, span):
             nc.tensor.matmul_mx(
                 out=dst, lhsT=lhs[0][:].bitcast(FP8X4), lhsT_scale=lhs[1][:],
-                rhs=rhs[0][:].bitcast(FP8X4), rhs_scale=rhs[1][:], start=True, stop=True,
+                rhs=rhs[0][:, span].bitcast(FP8X4), rhs_scale=rhs[1][:, span], start=True, stop=True,
             )
 
-        def store(j, sums):
-            res = sb.tile([P, P, 2], F32, name="res%d" % j)
-            nc.scalar.copy(res[:], sums[:, : 2 * P].rearrange("p (two m) -> p m two", two=2))
-            nc.sync.dma_start(out[:, j * 2 * P : (j + 1) * 2 * P], res[:].rearrange("p m two -> p (m two)"))
+        def planes(name, width, tag=None):
+            words = sb.tile([P, width], U32, name=name + "_words", tag=tag or name + "_words", align_bytes=64)
+            scales = sb.tile([P, width], U8, name=name + "_bytes", align_bytes=64)
+            return words, scales
 
-        cos0, sin0 = scaled_turn(0)
-        odd0 = gather("odd0", val_tab[0][ODD], tok_list)
-        q_mx = quantise("q", q_bf)
-        neg_odd0 = deal("neg_odd0", odd0, -1.0)
-        terms0 = odd_products(0, neg_odd0, deal("neg_cos0", cos0, -1.0), deal("sin_d0", sin0, 1.0))
+        def interleave(dst, acc):
+            nc.scalar.copy(dst, acc.rearrange("p (t c) -> p c t", t=PACK))
 
-        cos1, sin1 = scaled_turn(1)
-        neg_cos1 = deal("neg_cos1", cos1, -1.0)
-        sin_d1 = deal("sin_d1", sin1, 1.0)
+        size_ps = bank(6, "size_ps")
+        for t in range(PACK):
+            nc.tensor.transpose(size_ps[:, t * P : (t + 1) * P], cols[:, PACK + t : PACK + t + 1].to_broadcast([P, P]), ident[:])
+        q_bf = sb.tile([P, Q, PACK], BF16, name="q_bf", align_bytes=64)
+        nc.gpsimd.tensor_scalar(q_bf[:], q_raw[:].rearrange("p t q -> p q t"), 1.0, 0.0, ALU.mult, ALU.add)
+
+        cos0, sin0 = scaled_factors(0)
+        q_mx = planes("q", Q)
+        quantise(q_mx[0][:], q_mx[1][:], q_bf[:])
+        cos0_d = deal("cos0_d", cos0, 1.0)
+        neg_sin0_d = deal("neg_sin0_d", sin0, -1.0)
+        sin0_d = deal("sin0_d", sin0, 1.0)
+
+        odd0 = gather_dealt("odd0", val_tab[0][ODD])
+        odd_cos0 = pool_product("odd_cos0", odd0, cos0_d)
+        odd_sin0 = pool_product("odd_sin0", odd0, neg_sin0_d)
+
+        cos1, sin1 = scaled_factors(1)
+        acc0 = two_banks("acc0")
+        add_turned(acc0[ODD], odd_cos0, range(PACK), True)
+        add_turned(acc0[EVEN], odd_sin0, range(PACK), True)
+        cos1_d = deal("cos1_d", cos1, 1.0)
+        neg_sin1_d = deal("neg_sin1_d", sin1, -1.0)
+
+        even0 = gather_dealt("even0", val_tab[0][EVEN])
+        add_turned(acc0[EVEN], pool_product("even_cos0", even0, cos0_d), range(PACK), False)
+        add_turned(acc0[ODD], pool_product("even_sin0", even0, sin0_d), range(PACK), False)
+        v0_bf = sb.tile([P, 2 * P, PACK], BF16, name="v0_bf", align_bytes=64)
+        for par in range(2):
+            interleave(v0_bf[:, par * P : (par + 1) * P, :], acc0[par])
 
         k_mx = (gather("k_words", key_words, tok_list, U32), gather("k_bytes", key_bytes, tok_list, U8))
-        scores = bank(6, "scores")
-        product(scores[:], q_mx, k_mx)
+        scores = bank(7, "scores")
+        product(scores[:], q_mx, k_mx, slice(0, I))
 
-        odd1 = gather("odd1", val_tab[1][ODD], tok_list)
-        neg_odd1 = deal("neg_odd1", odd1, -1.0)
+        acc1 = [bank(2 + par, "acc1%d" % par)[:] for par in range(2)]
+        odd1 = gather_dealt("odd1", val_tab[1][ODD])
+        add_turned(acc1[ODD], pool_product("odd_cos1", odd1, cos1_d), range(PACK), True)
+        odd_sin1 = pool_product("odd_sin1", odd1, neg_sin1_d)
+
         neg_max = sb.tile([P, 1], F32, name="neg_max")
         nc.vector.tensor_reduce(neg_max[:], scores[:], AX.X, ALU.max, negate=True)
-        even0 = gather("even0", val_tab[0][EVEN], tok_list)
-        prob = sb.tile([P, I], F32, name="prob")
+        prob = sb.tile([P, I], F32, name="prob", align_bytes=64)
         total = sb.tile([P, 1], F32, name="total")
         nc.scalar.activation(by_place(prob[:]), dealt(scores[:]), ACT.Exp, bias=neg_max[:], scale=1.0, accum_out=total[:])
-        sized = sb.tile([P, I], F32, name="sized")
-        nc.gpsimd.tensor_tensor(sized[:], prob[:], size_all[:], ALU.mult)
-        terms1 = odd_products(1, neg_odd1, neg_cos1, sin_d1)
-        inv = sb.tile([P, 1], F32, name="inv")
+        even1 = gather("even1", val_tab[1][EVEN], tok_list, tag="k_words")
+
+        inv = sb.tile([P, 1], F32, name="inv", align_bytes=64)
         nc.vector.reciprocal(inv[:], total[:])
-        normed = sb.tile([P, I], F32, name="normed")
-        nc.scalar.activation(normed[:], sized[:], ACT.Copy, scale=inv[:])
         w_ps = bank(7, "w_ps")
-        for t in range(PACK):
-            nc.tensor.transpose(w_ps[:, t * P : (t + 1) * P], normed[:, t * P : (t + 1) * P], ident[:])
+        for u in range(2):
+            w_pairs = sb.tile([P, P, 2], BF16, name="w_pairs%d" % u, align_bytes=64)
+            span = slice(2 * u * P, 2 * (u + 1) * P)
+            nc.vector.scalar_tensor_tensor(
+                w_pairs[:], prob[:, span].rearrange("q (e p) -> q p e", e=2), inv[:],
+                size_ps[:, span].rearrange("q (e p) -> q p e", e=2), ALU.mult, ALU.mult,
+            )
+            nc.tensor.transpose(w_ps[:, u * P : (u + 1) * P], w_pairs[:].rearrange("q p e -> q (p e)").bitcast(F32), ident[:])
         w_bf = sb.tile([P, Q, PACK], BF16, name="w_bf", align_bytes=64)
-        nc.scalar.copy(w_bf[:], w_ps[:].rearrange("p (t q) -> p q t", t=PACK))
+        nc.scalar.copy(
+            w_bf[:].rearrange("p q t -> p (q t)").bitcast(F32).rearrange("p (q u) -> p q u", u=2),
+            w_ps[:, : 2 * P].rearrange("p (u q) -> p q u", u=2),
+        )
 
-        v01 = rotate(0, ODD, 0, terms0[ODD], even0, sin0, 1)
-        v00 = rotate(0, EVEN, 1, terms0[EVEN], even0, cos0, 1)
+        v1_bf = [sb.tile([P, P, PACK], BF16, name="v1_bf%d" % par, align_bytes=64) for par in range(2)]
+        vector_term("even_sin1", acc1[ODD], even1, sin1, 1, False, ["prob"])
+        interleave(v1_bf[ODD][:], acc1[ODD])
+        add_turned(acc1[EVEN], odd_sin1, range(PACK), True)
+        vector_term("even_cos1", acc1[EVEN], even1, cos1, 2, False, ["inv", "w_pairs0"])
+        interleave(v1_bf[EVEN][:], acc1[EVEN])
 
-        even1 = gather("even1", val_tab[1][EVEN], tok_list)
-        v11 = rotate(1, ODD, 3, terms1[ODD], even1, sin1, 1)
-        v10 = rotate(1, EVEN, 2, terms1[EVEN], even1, cos1, 2)
+        w_mx = planes("w", Q, tag="prob")
+        quantise(w_mx[0][:], w_mx[1][:], w_bf[:])
+        v0_mx = planes("v0", 2 * P, tag="k_words")
+        quantise(v0_mx[0][:], v0_mx[1][:], v0_bf[:])
+        sums = [bank(0, "sums0"), bank(4, "sums1")]
+        product(sums[0][:, : 2 * P], w_mx, v0_mx, slice(0, 2 * P))
+        v1_mx = planes("v1", 2 * P)
+        for par in (ODD, EVEN):
+            span = slice(par * P, (par + 1) * P)
+            quantise(v1_mx[0][:, span], v1_mx[1][:, span], v1_bf[par][:])
+            product(sums[1][:, span], w_mx, v1_mx, span)
 
-        w_mx = quantise("w", w_bf)
-        sums0 = bank(6, "sums0")
-        product(sums0[:, ODD * P : (ODD + 1) * P], w_mx, quantise("v01", v01))
-        product(sums0[:, EVEN * P : (EVEN + 1) * P], w_mx, quantise("v00", v00))
-        sums1 = bank(7, "sums1")
-        product(sums1[:, ODD * P : (ODD + 1) * P], w_mx, quantise("v11", v11))
-        store(0, sums0)
-        product(sums1[:, EVEN * P : (EVEN + 1) * P], w_mx, quantise("v10", v10))
-        store(1, sums1)
+        for j, copy in ((0, nc.scalar.copy), (1, nc.vector.tensor_copy)):
+            res = sb.tile([P, P, 2], F32, name="res%d" % j)
+            copy(res[:], sums[j][:, : 2 * P].rearrange("p (two m) -> p m two", two=2))
+            nc.sync.dma_start(out[:, j * 2 * P : (j + 1) * 2 * P], res[:].rearrange("p m two -> p (m two)"))

from contextlib import ExitStack

import concourse.mybir as mybir
from concourse.masks import make_identity

D, T, I, Q, E, U = 512, 1024, 512, 128, 512, 512
FLOPS = 2 * Q * D * I + 2 * Q * I * E

F32 = mybir.dt.float32
BF16 = mybir.dt.bfloat16
I32 = mybir.dt.int32
U32 = mybir.dt.uint32
U16 = mybir.dt.uint16
U8 = mybir.dt.uint8
FP8X4 = mybir.dt.float8_e4m3fn_x4
ALU = mybir.AluOpType
ACT = mybir.ActivationFunctionType
AX = mybir.AxisListType

P = 128
PACK = 4
RUN = 8
GROUPS = P // RUN
HALVES = 2
WINDOW = 704
EVEN, ODD = 0, 1


def dealt(ap):
    return ap.rearrange("p (g t r) -> p t g r", g=GROUPS, t=PACK, r=RUN)


def by_place(ap):
    return ap.rearrange("p (t g r) -> p t g r", g=GROUPS, t=PACK, r=RUN)


def tile_attend_turnedvalues_kernel(tc, query, keys_words, keys_scales, size, vals, cosn, sinn, vsc, offs, offs2, out):
    nc = tc.nc
    with ExitStack() as ctx:
        sb = ctx.enter_context(tc.tile_pool(name="sb", bufs=1))
        ps = ctx.enter_context(tc.psum_pool(name="ps", bufs=1))

        def bank(n, name):
            return ps.tile([P, 512], F32, tag="bank%d" % n, name=name)

        def two_banks(name):
            both = ps.tile([P, 2, 512], F32, tag="bank0", name=name)
            return [both[:, 0, :], both[:, 1, :]]

        tok_list = sb.tile([P, I // 16], U16, name="tok_list")
        dist_list = sb.tile([P, I // 16], U16, name="dist_list")
        cos_tab = [sb.tile([P, WINDOW], F32, name="cos_tab%d" % j, align_bytes=64) for j in range(HALVES)]
        sin_tab = [sb.tile([P, WINDOW], F32, name="sin_tab%d" % j, align_bytes=64) for j in range(HALVES)]
        val_tab = [[sb.tile([P, T], F32, name="val_tab%d%d" % (j, par), align_bytes=64) for par in range(2)] for j in range(HALVES)]
        key_words = sb.tile([P, T], U32, name="key_words", align_bytes=64)
        key_bytes = sb.tile([P, T], U8, name="key_bytes")
        q_raw = sb.tile([P, PACK, Q], F32, name="q_raw")
        rows = sb.tile([P, P], F32, name="rows")
        ident = sb.tile([P, P], F32, name="ident")
        warm = sb.tile([P, 1], F32, name="warm")
        warm_out = sb.tile([P, 1], F32, name="warm_out")

        nc.gpsimd.memset(rows[:], 0.0)
        nc.vector.memset(key_bytes[:].bitcast(I32), 0)
        for j in range(HALVES):
            nc.vector.memset(cos_tab[j][:, U:], 0.0)
            nc.vector.memset(sin_tab[j][:, U:], 0.0)
        nc.gpsimd.memset(warm[:], 0.0)
        make_identity(nc, ident[:])
        nc.scalar.activation(warm_out[:], warm[:], ACT.Exp)

        cos_rows = cosn.rearrange("(j p two) u -> j two p u", two=2, p=P)
        sin_rows = sinn.rearrange("(j p two) u -> j two p u", two=2, p=P)
        val_rows = vals.rearrange("(j p two) t -> j two p t", two=2, p=P)

        nc.sync.dma_start(dist_list[:], offs2)
        nc.sync.dma_start(cos_tab[0][:, :U], cos_rows[0, EVEN])
        nc.sync.dma_start(rows[0:PACK, :], vsc.rearrange("(b p) o -> b (p o)", p=P))
        nc.sync.dma_start(
            rows[PACK : 2 * PACK, :].rearrange("t (g r) -> t g r", r=RUN),
            size.rearrange("o (g t r) -> t (o g) r", t=PACK, r=RUN),
        )
        nc.sync.dma_start(sin_tab[0][:, :U], sin_rows[0, EVEN])
        nc.sync.dma_start(q_raw[:], query.rearrange("(p t) q -> p t q", t=PACK))
        nc.sync.dma_start(tok_list[:], offs)
        nc.sync.dma_start(val_tab[0][ODD][:], val_rows[0, ODD])
        nc.sync.dma_start(cos_tab[1][:, :U], cos_rows[1, EVEN])
        nc.sync.dma_start(sin_tab[1][:, :U], sin_rows[1, EVEN])
        nc.sync.dma_start(val_tab[0][EVEN][:], val_rows[0, EVEN])
        nc.sync.dma_start(key_words[:].bitcast(I32), keys_words[0].rearrange("p n t -> p (n t)").bitcast(I32))
        for quad in range(4):
            nc.sync.dma_start(
                key_bytes[32 * quad : 32 * quad + 4, :].bitcast(I32),
                keys_scales[0, 4 * quad : 4 * quad + 4, :].bitcast(I32),
            )
        nc.sync.dma_start(val_tab[1][ODD][:], val_rows[1, ODD])
        nc.sync.dma_start(val_tab[1][EVEN][:], val_rows[1, EVEN])

        cols_ps = bank(0, "cols_ps")
        nc.tensor.transpose(cols_ps[:, :P], rows[:], ident[:])
        cols = sb.tile([P, 2 * PACK], F32, name="cols")
        nc.scalar.copy(cols[:], cols_ps[:, : 2 * PACK])

        def gather(name, table, offsets, dtype=F32, tag=None):
            picked = sb.tile([P, I], dtype, name=name, tag=tag or name, align_bytes=64)
            nc.vector.tensor_copy(picked[:], table[:].indirect(offsets[:]))
            return picked

        def gather_dealt(name, table, tag=None):
            picked = sb.tile([P, I], F32, name=name, tag=tag or name, align_bytes=64)
            nc.vector.tensor_copy(
                picked[:].bitcast(U32).rearrange("p (t g r) -> p g t r", g=GROUPS, t=PACK, r=RUN),
                table[:].bitcast(U32).indirect(tok_list[:]),
            )
            return picked

        def scaled_factors(j):
            picked = [gather("cos%d" % j, cos_tab[j], dist_list), gather("sin%d" % j, sin_tab[j], dist_list)]
            there = two_banks("there%d" % j)
            for k in range(2):
                for b in range(PACK):
                    at = (2 * (b % 2) + k) * P
                    nc.tensor.transpose(there[b // 2][:, at : at + P], picked[k][:, b * P : (b + 1) * P], ident[:])
            back = [bank(2 + 2 * j + k, "back%d%d" % (j, k)) for k in range(2)]
            for b in range(PACK):
                scaled = sb.tile([P, 2 * P], F32, name="scaled%d%d" % (j, b))
                at = 2 * (b % 2) * P
                nc.scalar.activation(scaled[:], there[b // 2][:, at : at + 2 * P], ACT.Copy, scale=cols[:, b : b + 1])
                for k in range(2):
                    nc.tensor.transpose(back[k][:, b * P : (b + 1) * P], scaled[:, k * P : (k + 1) * P], ident[:])
            return back

        def deal(name, src, factor):
            dst = sb.tile([P, I], F32, name=name)
            nc.scalar.activation(by_place(dst[:]), dealt(src[:]), ACT.Copy, scale=factor)
            return dst

        def pool_product(name, a, b):
            prod = sb.tile([P, I], F32, name=name)
            nc.gpsimd.tensor_tensor(prod[:], a[:], b[:], ALU.mult)
            return prod

        def add_turned(acc, prod, places, first):
            for t in places:
                nc.tensor.matmul(
                    acc[:, t * P : (t + 1) * P], prod[:, t * P : (t + 1) * P], ident[:],
                    start=(first and t == 0), stop=(not first and t == PACK - 1), is_transpose=True,
                )

        def vector_term(name, acc, values, factor, cuts, first, tags):
            step = PACK // cuts
            for t0 in range(0, PACK, step):
                prod = sb.tile([P, I], F32, name="%s_%d" % (name, t0), tag=tags[t0 // step], align_bytes=64)
                nc.vector.tensor_tensor(
                    by_place(prod[:])[:, t0 : t0 + step], dealt(values[:])[:, t0 : t0 + step],
                    dealt(factor[:])[:, t0 : t0 + step], ALU.mult,
                )
                add_turned(acc, prod, range(t0, t0 + step), first)

        def quantise(words, scales, src):
            nc.vector.quantize_mx(out=words.bitcast(FP8X4), scales=scales, in_=src.rearrange("p c t -> p (c t)"))

        def product(dst, lhs, rhs, span):
            nc.tensor.matmul_mx(
                out=dst, lhsT=lhs[0][:].bitcast(FP8X4), lhsT_scale=lhs[1][:],
                rhs=rhs[0][:, span].bitcast(FP8X4), rhs_scale=rhs[1][:, span], start=True, stop=True,
            )

        def planes(name, width, tag=None):
            words = sb.tile([P, width], U32, name=name + "_words", tag=tag or name + "_words", align_bytes=64)
            scales = sb.tile([P, width], U8, name=name + "_bytes", align_bytes=64)
            return words, scales

        def interleave(dst, acc):
            nc.scalar.copy(dst, acc.rearrange("p (t c) -> p c t", t=PACK))

        size_ps = bank(6, "size_ps")
        for t in range(PACK):
            nc.tensor.transpose(size_ps[:, t * P : (t + 1) * P], cols[:, PACK + t : PACK + t + 1].to_broadcast([P, P]), ident[:])
        q_bf = sb.tile([P, Q, PACK], BF16, name="q_bf", align_bytes=64)
        nc.gpsimd.tensor_scalar(q_bf[:], q_raw[:].rearrange("p t q -> p q t"), 1.0, 0.0, ALU.mult, ALU.add)

        cos0, sin0 = scaled_factors(0)
        q_mx = planes("q", Q)
        quantise(q_mx[0][:], q_mx[1][:], q_bf[:])
        cos0_d = deal("cos0_d", cos0, 1.0)
        neg_sin0_d = deal("neg_sin0_d", sin0, -1.0)
        sin0_d = deal("sin0_d", sin0, 1.0)

        odd0 = gather_dealt("odd0", val_tab[0][ODD])
        odd_cos0 = pool_product("odd_cos0", odd0, cos0_d)
        odd_sin0 = pool_product("odd_sin0", odd0, neg_sin0_d)

        cos1, sin1 = scaled_factors(1)
        acc0 = two_banks("acc0")
        add_turned(acc0[ODD], odd_cos0, range(PACK), True)
        add_turned(acc0[EVEN], odd_sin0, range(PACK), True)
        cos1_d = deal("cos1_d", cos1, 1.0)
        neg_sin1_d = deal("neg_sin1_d", sin1, -1.0)

        even0 = gather_dealt("even0", val_tab[0][EVEN])
        add_turned(acc0[EVEN], pool_product("even_cos0", even0, cos0_d), range(PACK), False)
        add_turned(acc0[ODD], pool_product("even_sin0", even0, sin0_d), range(PACK), False)
        v0_bf = sb.tile([P, 2 * P, PACK], BF16, name="v0_bf", align_bytes=64)
        for par in range(2):
            interleave(v0_bf[:, par * P : (par + 1) * P, :], acc0[par])

        k_mx = (gather("k_words", key_words, tok_list, U32), gather("k_bytes", key_bytes, tok_list, U8))
        scores = bank(7, "scores")
        product(scores[:], q_mx, k_mx, slice(0, I))

        acc1 = [bank(2 + par, "acc1%d" % par)[:] for par in range(2)]
        odd1 = gather_dealt("odd1", val_tab[1][ODD])
        add_turned(acc1[ODD], pool_product("odd_cos1", odd1, cos1_d), range(PACK), True)
        odd_sin1 = pool_product("odd_sin1", odd1, neg_sin1_d)

        neg_max = sb.tile([P, 1], F32, name="neg_max")
        nc.vector.tensor_reduce(neg_max[:], scores[:], AX.X, ALU.max, negate=True)
        prob = sb.tile([P, I], F32, name="prob", align_bytes=64)
        total = sb.tile([P, 1], F32, name="total")
        nc.scalar.activation(by_place(prob[:]), dealt(scores[:]), ACT.Exp, bias=neg_max[:], scale=1.0, accum_out=total[:])
        even1 = gather("even1", val_tab[1][EVEN], tok_list, tag="k_words")

        inv = sb.tile([P, 1], F32, name="inv", align_bytes=64)
        nc.vector.reciprocal(inv[:], total[:])
        w_ps = bank(7, "w_ps")
        for u in range(2):
            w_pairs = sb.tile([P, P, 2], BF16, name="w_pairs%d" % u, align_bytes=64)
            span = slice(2 * u * P, 2 * (u + 1) * P)
            nc.vector.scalar_tensor_tensor(
                w_pairs[:], prob[:, span].rearrange("q (e p) -> q p e", e=2), inv[:],
                size_ps[:, span].rearrange("q (e p) -> q p e", e=2), ALU.mult, ALU.mult,
            )
            nc.tensor.transpose(w_ps[:, u * P : (u + 1) * P], w_pairs[:].rearrange("q p e -> q (p e)").bitcast(F32), ident[:])
        w_bf = sb.tile([P, Q, PACK], BF16, name="w_bf", align_bytes=64)
        nc.scalar.copy(
            w_bf[:].rearrange("p q t -> p (q t)").bitcast(F32).rearrange("p (q u) -> p q u", u=2),
            w_ps[:, : 2 * P].rearrange("p (u q) -> p q u", u=2),
        )

        v1_bf = [sb.tile([P, P, PACK], BF16, name="v1_bf%d" % par, align_bytes=64) for par in range(2)]
        vector_term("even_sin1", acc1[ODD], even1, sin1, 1, False, ["prob"])
        interleave(v1_bf[ODD][:], acc1[ODD])
        add_turned(acc1[EVEN], odd_sin1, range(PACK), True)
        vector_term("even_cos1", acc1[EVEN], even1, cos1, 2, False, ["inv", "w_pairs0"])
        interleave(v1_bf[EVEN][:], acc1[EVEN])

        w_mx = planes("w", Q, tag="prob")
        quantise(w_mx[0][:], w_mx[1][:], w_bf[:])
        v0_mx = planes("v0", 2 * P, tag="k_words")
        quantise(v0_mx[0][:], v0_mx[1][:], v0_bf[:])
        sums = [bank(0, "sums0"), bank(4, "sums1")]
        product(sums[0][:, : 2 * P], w_mx, v0_mx, slice(0, 2 * P))
        v1_mx = planes("v1", 2 * P)
        for par in (ODD, EVEN):
            span = slice(par * P, (par + 1) * P)
            quantise(v1_mx[0][:, span], v1_mx[1][:, span], v1_bf[par][:])
            product(sums[1][:, span], w_mx, v1_mx, span)

        for j, copy in ((0, nc.scalar.copy), (1, nc.vector.tensor_copy)):
            res = sb.tile([P, P, 2], F32, name="res%d" % j)
            copy(res[:], sums[j][:, : 2 * P].rearrange("p (two m) -> p m two", two=2))
            nc.sync.dma_start(out[:, j * 2 * P : (j + 1) * 2 * P], res[:].rearrange("p m two -> p (m two)"))
